import numpy as np
import ml_dtypes


def mxq(x, axis, fmt="e4m3"):
    dtype, down = {"e4m3": (ml_dtypes.float8_e4m3fn, 7), "e5m2": (ml_dtypes.float8_e5m2, 14)}[fmt]
    v = np.moveaxis(np.asarray(x, np.float32).astype(ml_dtypes.bfloat16).astype(np.float64), axis, -1)
    blocks = v.reshape(v.shape[:-1] + (-1, 32))
    amax = np.abs(blocks).max(-1, keepdims=True)
    byte = np.maximum(np.where(amax > 0, np.frexp(amax)[1] - 1 + 127, 0) - down, 1)
    scale = np.exp2(byte - 127.0)
    codes = (blocks / scale).astype(np.float32).astype(dtype).astype(np.float64)
    return np.moveaxis((codes * scale).reshape(v.shape), -1, axis)


WIDE = False


def mx_kscale(k, group=512):
    if not WIDE:
        return np.ones(k)
    levels = np.array([10, -10, 5, -5, 0])
    if group != 512:
        return np.exp2(np.random.permutation(np.resize(levels, k // group))).repeat(group)
    if k % 512:
        return np.exp2(np.random.permutation(np.resize(levels, k // 32))).repeat(32)
    a = np.empty((k // 512, 16))
    for p in range(k // 512):
        a[p, :8] = np.random.permutation(np.resize(levels, 8))
        for g in range(8):
            far = levels[np.abs(levels - a[p, g]) >= 10]
            a[p, g + 8] = far[np.random.randint(len(far))]
    return np.exp2(a.ravel()).repeat(32)


def f64(x):
    return np.asarray(x).astype(np.float64)


def sigmoid(v):
    return 1.0 / (1.0 + np.exp(-v))


def bf(x):
    return np.asarray(x, np.float32).astype(ml_dtypes.bfloat16)


def planes(Y):
    r, m = Y.shape
    b = f64(bf(Y)).reshape(r // 32, 32, m)
    amax = np.abs(b).max(1)
    byte = np.clip(np.where(amax > 0, np.frexp(amax)[1] - 1 + 127 - 7, 1), 1, 254)
    codes = (b * np.exp2(127.0 - byte)[:, None, :]).reshape(r, m).astype(np.float32).astype(ml_dtypes.float8_e4m3fn).view(np.uint8)
    words = codes.reshape(r // 512, 128, 4, m).transpose(0, 1, 3, 2)
    return np.ascontiguousarray(words), np.ascontiguousarray(byte.astype(np.uint8).reshape(r // 512, 16, m))


G, D, M, N = 2, 256, 256, 512


def setup_inputs():
    n = np.random.standard_normal
    s_d = mx_kscale(D, 0)
    return {
        "x": (n((G, D, N)) * s_d[:, None]).astype(np.float32),
        "w1": (n((G, D, M)) / np.sqrt(D) / s_d[:, None]).astype(np.float32),
        "w2": (n((G, D, M)) / np.sqrt(D) / s_d[:, None]).astype(np.float32),
        "th": (np.random.uniform(0.5, 1.5, (G, M, 1))).astype(np.float32),
        "dx": (n((G, D, N)) * s_d[:, None]).astype(np.float32),
        "og": (np.random.uniform(0.5, 2.0, (G, M, 1))).astype(np.float32),
        "base": (0.3 * n((G, M, N))).astype(np.float32),
    }


def reference(x, w1, w2, th, dx, og, base):
    w1q = mxq(f64(w1), 1, "e4m3")
    xq = mxq(f64(x), 1, "e4m3")
    z1 = w1q.transpose(0, 2, 1) @ xq
    dxq = mxq(f64(dx), 1, "e4m3")
    tz1 = w1q.transpose(0, 2, 1) @ dxq
    w2q = mxq(f64(w2), 1, "e4m3")
    z2 = w2q.transpose(0, 2, 1) @ xq
    tz2 = w2q.transpose(0, 2, 1) @ dxq
    mg = np.sqrt(np.square(z1) + np.square(z2) + 0.05)
    xmg = (tz1 * z1 * 2.0 + tz2 * z2 * 2.0) * 0.5 / mg
    xh = xmg * sigmoid(mg - f64(th)) + xmg * sigmoid(mg - f64(th)) * (1.0 - sigmoid(mg - f64(th))) * mg
    y = xh * f64(og) + f64(base)
    Y = y.reshape(G * M, N)
    words, scales = planes(Y)
    return Y, words, scales

@@ -1,0 +1,275 @@
+from contextlib import ExitStack
+
+import concourse.mybir as mybir
+
+G, D, M, N = 2, 256, 256, 512
+FLOPS = 4 * 2 * G * D * M * N
+
+F32 = mybir.dt.float32
+BF16 = mybir.dt.bfloat16
+I32 = mybir.dt.int32
+U32 = mybir.dt.uint32
+U8 = mybir.dt.uint8
+FP8X4 = mybir.dt.float8_e4m3fn_x4
+ACT = mybir.ActivationFunctionType
+ALU = mybir.AluOpType
+
+P = 128
+ROWS = 64
+PACK = 4
+COLS = 128
+HALVES = 2
+CHUNK = HALVES * COLS
+CHUNKS = N // CHUNK
+PAIRS = PACK // 2
+FLOOR = 0.05
+SLOTS = 2 * PACK + 1
+SCALAR_COLS = 96
+
+
+def tile_rows_pl_tnmagnitude_kernel(tc, x, w1, w2, th, dx, og, base, out_0, out_1, out_2):
+    nc = tc.nc
+    chunks = [(g, c) for c in range(CHUNKS) for g in range(G)]
+
+    def packed_rows(src):
+        return src.rearrange("g (p j) n -> (g p) j n", j=PACK)
+
+    def half(h):
+        return slice(ROWS * h, ROWS * (h + 1))
+
+    with ExitStack() as ctx:
+        sb = ctx.enter_context(tc.tile_pool(name="sb", bufs=1))
+        ps = ctx.enter_context(tc.psum_pool(name="ps", bufs=1))
+        ctx.enter_context(tc.manual_schedule())
+
+        def sbuf(name, shape, dtype):
+            return sb.tile(shape, dtype, name=name, align_bytes=64)
+
+        def per_chunk(name, shape):
+            return {(g, c): sbuf("%s_%d_%d" % (name, g, c), shape, F32) for g, c in chunks}
+
+        gain = sbuf("gain", [P, G, 8], F32)
+        thr = sbuf("thr", [P, G, 8], F32)
+        for dst, src in ((gain, og), (thr, th)):
+            for h in range(HALVES):
+                nc.scalar.dma_start(out=dst[half(h), :, 0:PACK], in_=src.rearrange("g (p t) o -> p g (t o)", t=PACK))
+        w_raw = [sbuf("w_raw%d" % k, [P, PACK, M], F32) for k in range(2)]
+        for k, src in enumerate((w1, w2)):
+            nc.sync.dma_start(out=w_raw[k][:], in_=packed_rows(src))
+        in_raw = {}
+        for name, src in (("x", x), ("dx", dx)):
+            for c in range(CHUNKS):
+                in_raw[name, c] = sbuf("%s_raw%d" % (name, c), [P, PACK, CHUNK], F32)
+                nc.sync.dma_start(out=in_raw[name, c][:], in_=packed_rows(src)[:, :, CHUNK * c : CHUNK * (c + 1)])
+        base_sb = [sbuf("base%d" % g, [P, PACK, CHUNKS, COLS], F32) for g in range(G)]
+        for g in range(G):
+            rows = base[g].rearrange("(p t) n -> p (t n)", t=PACK).rearrange("p (s h i) -> h p s i", h=HALVES, i=COLS)
+            for h in range(HALVES):
+                nc.sync.dma_start(out=base_sb[g][half(h)].rearrange("p t c i -> p (t c) i"), in_=rows[h])
+
+        warm_in = sbuf("warm_in", [P, 1], F32)
+        warm_out = sbuf("warm_out", [P, 1], F32)
+        nc.vector.memset(warm_in[:], 1.0)
+        nc.scalar.activation(out=warm_out[:], in_=warm_in[:], func=ACT.Abs_reciprocal_sqrt)
+
+        neg_thr = sbuf("neg_thr", [P, G, PACK], F32)
+        nc.gpsimd.tensor_scalar(out=neg_thr[:], in0=thr[:, :, 0:PACK], scalar1=-1.0, scalar2=0.0, op0=ALU.mult, op1=ALU.add)
+
+        w_codes = [sbuf("w_codes%d" % k, [P, SLOTS * ROWS], U32) for k in range(2)]
+        w_scales = [sbuf("w_scales%d" % k, [P, SLOTS * ROWS], U8) for k in range(2)]
+        w_bf = [sbuf("w_bf%d" % k, [P, PACK, ROWS * PACK], BF16) for k in range(2)]
+        for k in range(2):
+            nc.vector.memset(w_codes[k][:], 0)
+            nc.vector.memset(w_scales[k][:].bitcast(U32), 0)
+
+        def round_weights(k):
+            nc.vector.tensor_copy(
+                out=w_bf[k][:].rearrange("p (a b) (q j) -> p a q j b", b=2, j=PACK),
+                in_=w_raw[k][:].rearrange("p j (q a b) -> p a q j b", a=PAIRS, b=2),
+            )
+
+        def quantize_weights(k):
+            for t in range(PACK):
+                slot = slice(ROWS * (2 * t + 1), ROWS * (2 * t + 2))
+                nc.vector.quantize_mx(out=w_codes[k][:, slot].bitcast(FP8X4), scales=w_scales[k][:, slot], in_=w_bf[k][:, t, :])
+
+        def interleave(copy, dst, src, lo, hi):
+            copy(
+                out=dst[:, PACK * lo : PACK * hi].rearrange("p (c i j) -> p c j i", i=4, j=PACK),
+                in_=src[:, :, lo:hi].rearrange("p j (c i) -> p c j i", i=4),
+            )
+
+        in_bf = {key: sbuf("%s_bf%d" % key, [P, CHUNK * PACK], BF16) for key in in_raw}
+        in_codes = {key: sbuf("%s_codes%d" % key, [P, CHUNK], U32) for key in in_raw}
+        in_scales = {key: sbuf("%s_scales%d" % key, [P, CHUNK], U8) for key in in_raw}
+
+        def quantize_input(key):
+            nc.vector.quantize_mx(out=in_codes[key][:].bitcast(FP8X4), scales=in_scales[key][:], in_=in_bf[key][:])
+
+        banks = {(g, c, a): ps.tile([P, 2, 2, COLS], F32, name="bank_%d_%d_%d" % (g, c, a)) for g, c in chunks for a in range(PAIRS)}
+
+        def product_pass(name, g, c, a, b, k, h):
+            start = ROWS * (2 * (2 * a + b) + 1 - h)
+            window = slice(start, start + P)
+            cols = slice(COLS * h, COLS * (h + 1))
+            nc.tensor.matmul_mx(
+                out=banks[g, c, a][:, b, k, :],
+                lhsT=w_codes[k][half(g), window].bitcast(FP8X4),
+                lhsT_scale=w_scales[k][half(g), window],
+                rhs=in_codes[name, c][half(g), cols].bitcast(FP8X4),
+                rhs_scale=in_scales[name, c][half(g), cols],
+                start=(h == 0),
+                stop=(h == HALVES - 1),
+            )
+
+        passes = [(b, k, h) for b in range(2) for k in range(2) for h in range(HALVES)]
+
+        def z_products(c):
+            for a in range(PAIRS):
+                for b, k, h in passes:
+                    for g in range(G):
+                        product_pass("x", g, c, a, b, k, h)
+
+        def dz_products(g, c, a):
+            for b, k, h in passes:
+                product_pass("dx", g, c, a, b, k, h)
+
+        sq = per_chunk("sq", [P, PACK, 2, COLS])
+        zg = per_chunk("zg", [P, PACK, 2, COLS])
+        prod = per_chunk("prod", [P, PACK, 2, COLS])
+        ssq = per_chunk("ssq", [P, PACK, COLS])
+        inv = per_chunk("inv", [P, PACK, COLS])
+        mag = per_chunk("mag", [P, PACK, COLS])
+        num = per_chunk("num", [P, PACK, COLS])
+        gate = per_chunk("gate", [P, PACK, COLS])
+        rest = per_chunk("rest", [P, PACK, COLS])
+        numg = per_chunk("numg", [P, PACK, COLS])
+        change = per_chunk("change", [P, PACK, COLS])
+        y = per_chunk("y", [P, PACK, COLS])
+        y_bf = {key: sbuf("y_bf%d_%d" % key, [P, COLS * PACK], BF16) for key in chunks}
+        y_codes = [sbuf("y_codes%d" % c, [P, G, COLS], U32) for c in range(CHUNKS)]
+        y_scales = [sbuf("y_scales%d" % c, [P, G, COLS], U8) for c in range(CHUNKS)]
+
+        def square(g, c, a):
+            nc.scalar.activation(out=sq[g, c][:, 2 * a : 2 * a + 2], in_=banks[g, c, a][:], func=ACT.Square)
+
+        def scale_z(g, c, a):
+            for b in range(2):
+                t = 2 * a + b
+                nc.scalar.activation(out=zg[g, c][:, t], in_=banks[g, c, a][:, b], func=ACT.Copy, scale=gain[:, g, t : t + 1])
+            dz_products(g, c, a)
+
+        def sum_squares(key):
+            nc.vector.scalar_tensor_tensor(out=ssq[key][:], in0=sq[key][:, :, 0, :], scalar=FLOOR, in1=sq[key][:, :, 1, :], op0=ALU.add, op1=ALU.add)
+
+        def inverse_root(key):
+            nc.scalar.activation(out=inv[key][:], in_=ssq[key][:], func=ACT.Abs_reciprocal_sqrt)
+
+        def magnitude(key):
+            nc.vector.tensor_tensor(out=mag[key][:], in0=ssq[key][:], in1=inv[key][:], op=ALU.mult)
+
+        def cross(g, c, a):
+            pair = slice(2 * a, 2 * a + 2)
+            nc.vector.tensor_tensor(out=prod[g, c][:, pair], in0=banks[g, c, a][:], in1=zg[g, c][:, pair], op=ALU.mult)
+
+        def numerator(key):
+            nc.vector.tensor_tensor(out=num[key][:], in0=prod[key][:, :, 0, :], in1=prod[key][:, :, 1, :], op=ALU.add)
+
+        def sigmoid(key):
+            g = key[0]
+            for t in range(PACK):
+                nc.scalar.activation(out=gate[key][:, t], in_=mag[key][:, t], func=ACT.Sigmoid, bias=neg_thr[:, g, t : t + 1])
+
+        def rest_factor(key):
+            nc.vector.scalar_tensor_tensor(out=rest[key][:], in0=inv[key][:], scalar=1.0, in1=gate[key][:], op0=ALU.add, op1=ALU.subtract)
+
+        def gated_numerator(key):
+            nc.vector.tensor_tensor(out=numg[key][:], in0=num[key][:], in1=gate[key][:], op=ALU.mult)
+
+        def gated_change(key):
+            nc.vector.tensor_tensor(out=change[key][:], in0=numg[key][:], in1=rest[key][:], op=ALU.mult)
+
+        def add_base(key):
+            g, c = key
+            nc.vector.tensor_tensor(out=y[key][:], in0=change[key][:], in1=base_sb[g][:, :, c, :], op=ALU.add)
+            rows = out_0.rearrange("(g p t) (c h i) -> g c h p t i", g=G, t=PACK, c=CHUNKS, h=HALVES)
+            for h in range(HALVES):
+                nc.sync.dma_start(out=rows[g, c, h], in_=y[key][half(h)])
+
+        def quantize_result(key):
+            g, c = key
+            nc.vector.quantize_mx(out=y_codes[c][:, g].bitcast(FP8X4), scales=y_scales[c][:, g], in_=y_bf[key][:])
+
+        def store_planes(c, scale_queue):
+            words = out_1[0].rearrange("p n u -> p (n u)").bitcast(I32).rearrange("(g p) (c h i) -> c h p g i", g=G, c=CHUNKS, h=HALVES)
+            for h in range(HALVES):
+                nc.sync.dma_start(out=words[c, h], in_=y_codes[c][half(h)].bitcast(I32))
+            rows = out_2[0].bitcast(I32).rearrange("(g q r) (c h i) -> c h q r g i", g=G, q=2, c=CHUNKS, h=HALVES)
+            for h in range(HALVES):
+                for q in range(2):
+                    first = ROWS * h + 32 * q
+                    scale_queue.dma_start(out=rows[c, h, q], in_=y_scales[c][first : first + 4].bitcast(I32))
+
+        round_weights(0)
+        quantize_weights(0)
+        round_weights(1)
+        quantize_weights(1)
+        interleave(nc.scalar.copy, in_bf["x", 0], in_raw["x", 0], 0, SCALAR_COLS)
+        interleave(nc.vector.tensor_copy, in_bf["x", 0], in_raw["x", 0], SCALAR_COLS, CHUNK)
+        quantize_input(("x", 0))
+        z_products(0)
+        for key in (("x", 1), ("dx", 0), ("dx", 1)):
+            interleave(nc.vector.tensor_copy, in_bf[key], in_raw[key], 0, CHUNK)
+            quantize_input(key)
+        z_products(1)
+
+        for c in range(CHUNKS):
+            for a in range(PAIRS):
+                for g in range(G):
+                    square(g, c, a)
+            for g in range(G):
+                sum_squares((g, c))
+            for g in range(G):
+                scale_z(g, c, 0)
+                inverse_root((g, c))
+            for g in range(G):
+                scale_z(g, c, 1)
+            for g in range(G):
+                magnitude((g, c))
+                cross(g, c, 0)
+            for g in range(G):
+                cross(g, c, 1)
+            for g in range(G):
+                numerator((g, c))
+
+        first, second, third, last = chunks
+        sigmoid(first)
+        sigmoid(second)
+        sigmoid(third)
+        sigmoid(last)
+        rest_factor(first)
+        gated_numerator(first)
+        rest_factor(second)
+        gated_change(first)
+        gated_numerator(second)
+        add_base(first)
+        interleave(nc.scalar.copy, y_bf[first], y[first], 0, COLS)
+        gated_change(second)
+        rest_factor(third)
+        add_base(second)
+        interleave(nc.scalar.copy, y_bf[second], y[second], 0, COLS)
+        gated_numerator(third)
+        rest_factor(last)
+        gated_change(third)
+        gated_numerator(last)
+        add_base(third)
+        interleave(nc.scalar.copy, y_bf[third], y[third], 0, COLS)
+        quantize_result(first)
+        gated_change(last)
+        quantize_result(second)
+        store_planes(0, nc.sync)
+        add_base(last)
+        quantize_result(third)
+        interleave(nc.vector.tensor_copy, y_bf[last], y[last], 0, COLS)
+        quantize_result(last)
+        store_planes(1, nc.scalar)

@@ -24,7 +24,8 @@ CHUNKS = N // CHUNK
 PAIRS = PACK // 2
 FLOOR = 0.05
 SLOTS = 2 * PACK + 1
-SCALAR_COLS = 96
+SCALAR_COLS = 88
+SCALAR_Q = 20
 
 
 def tile_rows_pl_tnmagnitude_kernel(tc, x, w1, w2, th, dx, og, base, out_0, out_1, out_2):
@@ -46,7 +47,7 @@ def tile_rows_pl_tnmagnitude_kernel(tc, x, w1, w2, th, dx, og, base, out_0, out_
             return sb.tile(shape, dtype, name=name, align_bytes=64)
 
         def per_chunk(name, shape):
-            return {(g, c): sbuf("%s_%d_%d" % (name, g, c), shape, F32) for g, c in chunks}
+            return [sbuf("%s%d" % (name, c), [P, G, PACK] + shape, F32) for c in range(CHUNKS)]
 
         gain = sbuf("gain", [P, G, 8], F32)
         thr = sbuf("thr", [P, G, 8], F32)
@@ -54,18 +55,22 @@ def tile_rows_pl_tnmagnitude_kernel(tc, x, w1, w2, th, dx, og, base, out_0, out_
             for h in range(HALVES):
                 nc.scalar.dma_start(out=dst[half(h), :, 0:PACK], in_=src.rearrange("g (p t) o -> p g (t o)", t=PACK))
         w_raw = [sbuf("w_raw%d" % k, [P, PACK, M], F32) for k in range(2)]
-        for k, src in enumerate((w1, w2)):
-            nc.sync.dma_start(out=w_raw[k][:], in_=packed_rows(src))
-        in_raw = {}
-        for name, src in (("x", x), ("dx", dx)):
-            for c in range(CHUNKS):
-                in_raw[name, c] = sbuf("%s_raw%d" % (name, c), [P, PACK, CHUNK], F32)
-                nc.sync.dma_start(out=in_raw[name, c][:], in_=packed_rows(src)[:, :, CHUNK * c : CHUNK * (c + 1)])
-        base_sb = [sbuf("base%d" % g, [P, PACK, CHUNKS, COLS], F32) for g in range(G)]
+        in_raw = {(name, c): sbuf("%s_raw%d" % (name, c), [P, PACK, CHUNK], F32) for name in ("x", "dx") for c in range(CHUNKS)}
+
+        def load_input(name, src, c):
+            nc.sync.dma_start(out=in_raw[name, c][:], in_=packed_rows(src)[:, :, CHUNK * c : CHUNK * (c + 1)])
+
+        nc.sync.dma_start(out=w_raw[0][:], in_=packed_rows(w1))
+        load_input("x", x, 0)
+        nc.sync.dma_start(out=w_raw[1][:], in_=packed_rows(w2))
+        load_input("dx", dx, 0)
+        load_input("x", x, 1)
+        load_input("dx", dx, 1)
+        base_sb = sbuf("base", [P, G, PACK, CHUNKS, COLS], F32)
         for g in range(G):
             rows = base[g].rearrange("(p t) n -> p (t n)", t=PACK).rearrange("p (s h i) -> h p s i", h=HALVES, i=COLS)
             for h in range(HALVES):
-                nc.sync.dma_start(out=base_sb[g][half(h)].rearrange("p t c i -> p (t c) i"), in_=rows[h])
+                nc.sync.dma_start(out=base_sb[half(h), g].rearrange("p t c i -> p (t c) i"), in_=rows[h])
 
         warm_in = sbuf("warm_in", [P, 1], F32)
         warm_out = sbuf("warm_out", [P, 1], F32)
@@ -73,7 +78,6 @@ def tile_rows_pl_tnmagnitude_kernel(tc, x, w1, w2, th, dx, og, base, out_0, out_
         nc.scalar.activation(out=warm_out[:], in_=warm_in[:], func=ACT.Abs_reciprocal_sqrt)
 
         neg_thr = sbuf("neg_thr", [P, G, PACK], F32)
-        nc.gpsimd.tensor_scalar(out=neg_thr[:], in0=thr[:, :, 0:PACK], scalar1=-1.0, scalar2=0.0, op0=ALU.mult, op1=ALU.add)
 
         w_codes = [sbuf("w_codes%d" % k, [P, SLOTS * ROWS], U32) for k in range(2)]
         w_scales = [sbuf("w_scales%d" % k, [P, SLOTS * ROWS], U8) for k in range(2)]
@@ -83,10 +87,10 @@ def tile_rows_pl_tnmagnitude_kernel(tc, x, w1, w2, th, dx, og, base, out_0, out_
             nc.vector.memset(w_scales[k][:].bitcast(U32), 0)
 
         def round_weights(k):
-            nc.vector.tensor_copy(
-                out=w_bf[k][:].rearrange("p (a b) (q j) -> p a q j b", b=2, j=PACK),
-                in_=w_raw[k][:].rearrange("p j (q a b) -> p a q j b", a=PAIRS, b=2),
-            )
+            dst = w_bf[k][:].rearrange("p (a b) (q j) -> p a q j b", b=2, j=PACK)
+            src = w_raw[k][:].rearrange("p j (q a b) -> p a q j b", a=PAIRS, b=2)
+            nc.scalar.copy(out=dst[:, :, 0:SCALAR_Q], in_=src[:, :, 0:SCALAR_Q])
+            nc.vector.tensor_copy(out=dst[:, :, SCALAR_Q:], in_=src[:, :, SCALAR_Q:])
 
         def quantize_weights(k):
             for t in range(PACK):
@@ -122,154 +126,211 @@ def tile_rows_pl_tnmagnitude_kernel(tc, x, w1, w2, th, dx, og, base, out_0, out_
                 stop=(h == HALVES - 1),
             )
 
-        passes = [(b, k, h) for b in range(2) for k in range(2) for h in range(HALVES)]
+        passes = [(k, b, h) for k in range(2) for b in range(2) for h in range(HALVES)]
 
-        def z_products(c):
-            for a in range(PAIRS):
-                for b, k, h in passes:
-                    for g in range(G):
-                        product_pass("x", g, c, a, b, k, h)
+        def products(name, c, a):
+            for k, b, h in passes:
+                for g in range(G):
+                    product_pass(name, g, c, a, b, k, h)
 
-        def dz_products(g, c, a):
-            for b, k, h in passes:
-                product_pass("dx", g, c, a, b, k, h)
-
-        sq = per_chunk("sq", [P, PACK, 2, COLS])
-        zg = per_chunk("zg", [P, PACK, 2, COLS])
-        prod = per_chunk("prod", [P, PACK, 2, COLS])
-        ssq = per_chunk("ssq", [P, PACK, COLS])
-        inv = per_chunk("inv", [P, PACK, COLS])
-        mag = per_chunk("mag", [P, PACK, COLS])
-        num = per_chunk("num", [P, PACK, COLS])
-        gate = per_chunk("gate", [P, PACK, COLS])
-        rest = per_chunk("rest", [P, PACK, COLS])
-        numg = per_chunk("numg", [P, PACK, COLS])
-        change = per_chunk("change", [P, PACK, COLS])
-        y = per_chunk("y", [P, PACK, COLS])
-        y_bf = {key: sbuf("y_bf%d_%d" % key, [P, COLS * PACK], BF16) for key in chunks}
+        sq = per_chunk("sq", [2, COLS])
+        zg = per_chunk("zg", [2, COLS])
+        prod = per_chunk("prod", [2, COLS])
+        ssq = per_chunk("ssq", [COLS])
+        inv = per_chunk("inv", [COLS])
+        mag = per_chunk("mag", [COLS])
+        num = per_chunk("num", [COLS])
+        gate = per_chunk("gate", [COLS])
+        rest = per_chunk("rest", [COLS])
+        numg = per_chunk("numg", [COLS])
+        change = per_chunk("change", [COLS])
+        y = per_chunk("y", [COLS])
+        y_bf = [sbuf("y_bf%d" % c, [P, G, COLS * PACK], BF16) for c in range(CHUNKS)]
         y_codes = [sbuf("y_codes%d" % c, [P, G, COLS], U32) for c in range(CHUNKS)]
         y_scales = [sbuf("y_scales%d" % c, [P, G, COLS], U8) for c in range(CHUNKS)]
 
-        def square(g, c, a):
-            nc.scalar.activation(out=sq[g, c][:, 2 * a : 2 * a + 2], in_=banks[g, c, a][:], func=ACT.Square)
+        def by_pair(c, a):
+            return (c, slice(0, G), slice(2 * a, 2 * a + 2), slice(0, COLS))
+
+        def by_group(c, g, lo=0, hi=COLS):
+            return (c, slice(g, g + 1), slice(0, PACK), slice(lo, hi))
+
+        def view(tiles, part):
+            c, gs, ts, cols = part
+            return tiles[c][:, gs, ts, cols]
+
+        def term(tiles, part, k):
+            c, gs, ts, cols = part
+            return tiles[c][:, gs, ts, k, cols]
+
+        def square(c, a):
+            for g in range(G):
+                nc.scalar.activation(out=sq[c][:, g, 2 * a : 2 * a + 2], in_=banks[g, c, a][:], func=ACT.Square)
 
         def scale_z(g, c, a):
             for b in range(2):
                 t = 2 * a + b
-                nc.scalar.activation(out=zg[g, c][:, t], in_=banks[g, c, a][:, b], func=ACT.Copy, scale=gain[:, g, t : t + 1])
-            dz_products(g, c, a)
+                nc.scalar.activation(out=zg[c][:, g, t], in_=banks[g, c, a][:, b], func=ACT.Copy, scale=gain[:, g, t : t + 1])
 
-        def sum_squares(key):
-            nc.vector.scalar_tensor_tensor(out=ssq[key][:], in0=sq[key][:, :, 0, :], scalar=FLOOR, in1=sq[key][:, :, 1, :], op0=ALU.add, op1=ALU.add)
+        def sum_squares(part):
+            nc.vector.tensor_tensor(out=view(ssq, part), in0=term(sq, part, 0), in1=term(sq, part, 1), op=ALU.add)
 
-        def inverse_root(key):
-            nc.scalar.activation(out=inv[key][:], in_=ssq[key][:], func=ACT.Abs_reciprocal_sqrt)
+        def inverse_root(part):
+            nc.scalar.activation(out=view(inv, part), in_=view(ssq, part), func=ACT.Abs_reciprocal_sqrt, bias=FLOOR)
 
-        def magnitude(key):
-            nc.vector.tensor_tensor(out=mag[key][:], in0=ssq[key][:], in1=inv[key][:], op=ALU.mult)
+        def magnitude(part):
+            nc.vector.scalar_tensor_tensor(out=view(mag, part), in0=view(ssq, part), scalar=FLOOR, in1=view(inv, part), op0=ALU.add, op1=ALU.mult)
 
         def cross(g, c, a):
             pair = slice(2 * a, 2 * a + 2)
-            nc.vector.tensor_tensor(out=prod[g, c][:, pair], in0=banks[g, c, a][:], in1=zg[g, c][:, pair], op=ALU.mult)
+            nc.vector.tensor_tensor(out=prod[c][:, g, pair], in0=banks[g, c, a][:], in1=zg[c][:, g, pair], op=ALU.mult)
 
-        def numerator(key):
-            nc.vector.tensor_tensor(out=num[key][:], in0=prod[key][:, :, 0, :], in1=prod[key][:, :, 1, :], op=ALU.add)
+        def numerator(part):
+            nc.vector.tensor_tensor(out=view(num, part), in0=term(prod, part, 0), in1=term(prod, part, 1), op=ALU.add)
 
-        def sigmoid(key):
-            g = key[0]
-            for t in range(PACK):
-                nc.scalar.activation(out=gate[key][:, t], in_=mag[key][:, t], func=ACT.Sigmoid, bias=neg_thr[:, g, t : t + 1])
+        def sigmoid(part):
+            c, gs, ts, cols = part
+            for g in range(gs.start, gs.stop):
+                for t in range(ts.start, ts.stop):
+                    nc.scalar.activation(out=gate[c][:, g, t], in_=mag[c][:, g, t], func=ACT.Sigmoid, bias=neg_thr[:, g, t : t + 1])
 
-        def rest_factor(key):
-            nc.vector.scalar_tensor_tensor(out=rest[key][:], in0=inv[key][:], scalar=1.0, in1=gate[key][:], op0=ALU.add, op1=ALU.subtract)
+        def rest_factor(part):
+            nc.vector.scalar_tensor_tensor(out=view(rest, part), in0=view(inv, part), scalar=1.0, in1=view(gate, part), op0=ALU.add, op1=ALU.subtract)
 
-        def gated_numerator(key):
-            nc.vector.tensor_tensor(out=numg[key][:], in0=num[key][:], in1=gate[key][:], op=ALU.mult)
+        def gated_numerator(part):
+            nc.vector.tensor_tensor(out=view(numg, part), in0=view(num, part), in1=view(gate, part), op=ALU.mult)
 
-        def gated_change(key):
-            nc.vector.tensor_tensor(out=change[key][:], in0=numg[key][:], in1=rest[key][:], op=ALU.mult)
+        def gated_change(part):
+            nc.vector.tensor_tensor(out=view(change, part), in0=view(numg, part), in1=view(rest, part), op=ALU.mult)
 
-        def add_base(key):
-            g, c = key
-            nc.vector.tensor_tensor(out=y[key][:], in0=change[key][:], in1=base_sb[g][:, :, c, :], op=ALU.add)
+        def add_base(part):
+            c, gs, ts, cols = part
+            nc.vector.tensor_tensor(out=view(y, part), in0=view(change, part), in1=base_sb[:, gs, ts, c, cols], op=ALU.add)
+
+        def store_result(c, g, queues):
             rows = out_0.rearrange("(g p t) (c h i) -> g c h p t i", g=G, t=PACK, c=CHUNKS, h=HALVES)
             for h in range(HALVES):
-                nc.sync.dma_start(out=rows[g, c, h], in_=y[key][half(h)])
+                queues[h].dma_start(out=rows[g, c, h], in_=y[c][half(h), g])
 
-        def quantize_result(key):
-            g, c = key
-            nc.vector.quantize_mx(out=y_codes[c][:, g].bitcast(FP8X4), scales=y_scales[c][:, g], in_=y_bf[key][:])
+        def round_result(copy, c, g, lo=0, hi=COLS):
+            interleave(copy, y_bf[c][:, g], y[c][:, g], lo, hi)
 
-        def store_planes(c, scale_queue):
+        def quantize_result(c, g):
+            nc.vector.quantize_mx(out=y_codes[c][:, g].bitcast(FP8X4), scales=y_scales[c][:, g], in_=y_bf[c][:, g])
+
+        def store_planes(c, queues):
             words = out_1[0].rearrange("p n u -> p (n u)").bitcast(I32).rearrange("(g p) (c h i) -> c h p g i", g=G, c=CHUNKS, h=HALVES)
             for h in range(HALVES):
-                nc.sync.dma_start(out=words[c, h], in_=y_codes[c][half(h)].bitcast(I32))
+                queues[h].dma_start(out=words[c, h], in_=y_codes[c][half(h)].bitcast(I32))
             rows = out_2[0].bitcast(I32).rearrange("(g q r) (c h i) -> c h q r g i", g=G, q=2, c=CHUNKS, h=HALVES)
             for h in range(HALVES):
                 for q in range(2):
                     first = ROWS * h + 32 * q
-                    scale_queue.dma_start(out=rows[c, h, q], in_=y_scales[c][first : first + 4].bitcast(I32))
+                    queues[h].dma_start(out=rows[c, h, q], in_=y_scales[c][first : first + 4].bitcast(I32))
+
+        both = (nc.sync, nc.scalar)
+        one = (nc.sync, nc.sync)
+
+        def round_input(key, split):
+            if split:
+                interleave(nc.scalar.copy, in_bf[key], in_raw[key], 0, split)
+            interleave(nc.vector.tensor_copy, in_bf[key], in_raw[key], split, CHUNK)
 
         round_weights(0)
         quantize_weights(0)
+        round_input(("x", 0), SCALAR_COLS)
+        quantize_input(("x", 0))
         round_weights(1)
         quantize_weights(1)
-        interleave(nc.scalar.copy, in_bf["x", 0], in_raw["x", 0], 0, SCALAR_COLS)
-        interleave(nc.vector.tensor_copy, in_bf["x", 0], in_raw["x", 0], SCALAR_COLS, CHUNK)
-        quantize_input(("x", 0))
-        z_products(0)
-        for key in (("x", 1), ("dx", 0), ("dx", 1)):
-            interleave(nc.vector.tensor_copy, in_bf[key], in_raw[key], 0, CHUNK)
-            quantize_input(key)
-        z_products(1)
 
-        for c in range(CHUNKS):
-            for a in range(PAIRS):
-                for g in range(G):
-                    square(g, c, a)
-            for g in range(G):
-                sum_squares((g, c))
-            for g in range(G):
-                scale_z(g, c, 0)
-                inverse_root((g, c))
-            for g in range(G):
-                scale_z(g, c, 1)
-            for g in range(G):
-                magnitude((g, c))
-                cross(g, c, 0)
-            for g in range(G):
-                cross(g, c, 1)
-            for g in range(G):
-                numerator((g, c))
+        early = [by_pair(0, a) for a in range(PAIRS)]
+        late = [by_pair(1, a) for a in range(PAIRS)]
+        third, last = by_group(1, 0), by_group(1, 1)
+        last_halves = [by_group(1, 1, 0, COLS // 2), by_group(1, 1, COLS // 2, COLS)]
 
-        first, second, third, last = chunks
-        sigmoid(first)
-        sigmoid(second)
+        def both_groups(step, c, a):
+            for g in range(G):
+                step(g, c, a)
+
+        products("x", 0, 0)
+        products("x", 0, 1)
+        round_input(("dx", 0), SCALAR_COLS)
+        quantize_input(("dx", 0))
+        round_input(("x", 1), 0)
+        nc.scalar.activation(out=neg_thr[:], in_=thr[:, :, 0:PACK], func=ACT.Copy, scale=-1.0)
+        square(0, 0)
+        both_groups(scale_z, 0, 0)
+        products("dx", 0, 0)
+        quantize_input(("x", 1))
+        products("x", 1, 0)
+        products("x", 1, 1)
+        sum_squares(early[0])
+        round_input(("dx", 1), 0)
+        quantize_input(("dx", 1))
+        square(0, 1)
+        inverse_root(early[0])
+        sum_squares(early[1])
+        magnitude(early[0])
+        inverse_root(early[1])
+        both_groups(cross, 0, 0)
+        magnitude(early[1])
+        numerator(early[0])
+        sigmoid(early[0])
+        both_groups(scale_z, 0, 1)
+        products("dx", 0, 1)
+        sigmoid(early[1])
+        square(1, 0)
+        both_groups(scale_z, 1, 0)
+        products("dx", 1, 0)
+        square(1, 1)
+        both_groups(scale_z, 1, 1)
+        products("dx", 1, 1)
+        rest_factor(early[0])
+        gated_numerator(early[0])
+        gated_change(early[0])
+        rest_factor(early[1])
+        add_base(early[0])
+        sum_squares(late[0])
+        both_groups(cross, 0, 1)
+        sum_squares(late[1])
+        numerator(early[1])
+        inverse_root(late[0])
+        inverse_root(late[1])
+        cross(0, 1, 0)
+        gated_numerator(early[1])
+        cross(1, 1, 0)
+        gated_change(early[1])
+        numerator(late[0])
+        add_base(early[1])
+        store_result(0, 0, one)
+        store_result(0, 1, one)
+        magnitude(late[0])
+        magnitude(late[1])
         sigmoid(third)
         sigmoid(last)
-        rest_factor(first)
-        gated_numerator(first)
-        rest_factor(second)
-        gated_change(first)
-        gated_numerator(second)
-        add_base(first)
-        interleave(nc.scalar.copy, y_bf[first], y[first], 0, COLS)
-        gated_change(second)
+        round_result(nc.scalar.copy, 0, 0)
+        round_result(nc.scalar.copy, 0, 1)
+        both_groups(cross, 1, 1)
         rest_factor(third)
-        add_base(second)
-        interleave(nc.scalar.copy, y_bf[second], y[second], 0, COLS)
-        gated_numerator(third)
+        numerator(late[1])
         rest_factor(last)
+        gated_numerator(third)
+        quantize_result(0, 0)
         gated_change(third)
-        gated_numerator(last)
+        quantize_result(0, 1)
+        store_planes(0, one)
         add_base(third)
-        interleave(nc.scalar.copy, y_bf[third], y[third], 0, COLS)
-        quantize_result(first)
-        gated_change(last)
-        quantize_result(second)
-        store_planes(0, nc.sync)
-        add_base(last)
-        quantize_result(third)
-        interleave(nc.vector.tensor_copy, y_bf[last], y[last], 0, COLS)
-        quantize_result(last)
-        store_planes(1, nc.scalar)
+        store_result(1, 0, both)
+        round_result(nc.scalar.copy, 1, 0)
+        for part in last_halves:
+            gated_numerator(part)
+        for part in last_halves:
+            gated_change(part)
+        add_base(last_halves[0])
+        round_result(nc.scalar.copy, 1, 1, 0, COLS // 2)
+        add_base(last_halves[1])
+        quantize_result(1, 0)
+        round_result(nc.vector.tensor_copy, 1, 1, COLS // 2, COLS)
+        store_result(1, 1, both)
+        quantize_result(1, 1)
+        store_planes(1, both)

@@ -51,9 +51,11 @@ def tile_rows_pl_tnmagnitude_kernel(tc, x, w1, w2, th, dx, og, base, out_0, out_
 
         gain = sbuf("gain", [P, G, 8], F32)
         thr = sbuf("thr", [P, G, 8], F32)
-        for dst, src in ((gain, og), (thr, th)):
+
+        def load_per_row(queue, dst, src):
             for h in range(HALVES):
-                nc.scalar.dma_start(out=dst[half(h), :, 0:PACK], in_=src.rearrange("g (p t) o -> p g (t o)", t=PACK))
+                queue.dma_start(out=dst[half(h), :, 0:PACK], in_=src.rearrange("g (p t) o -> p g (t o)", t=PACK))
+
         w_raw = [sbuf("w_raw%d" % k, [P, PACK, M], F32) for k in range(2)]
         in_raw = {(name, c): sbuf("%s_raw%d" % (name, c), [P, PACK, CHUNK], F32) for name in ("x", "dx") for c in range(CHUNKS)}
 
@@ -63,11 +65,13 @@ def tile_rows_pl_tnmagnitude_kernel(tc, x, w1, w2, th, dx, og, base, out_0, out_
         nc.sync.dma_start(out=w_raw[0][:], in_=packed_rows(w1))
         load_input("x", x, 0)
         nc.sync.dma_start(out=w_raw[1][:], in_=packed_rows(w2))
-        load_input("dx", dx, 0)
+        load_per_row(nc.sync, gain, og)
         load_input("x", x, 1)
+        load_input("dx", dx, 0)
         load_input("dx", dx, 1)
         base_sb = sbuf("base", [P, G, PACK, CHUNKS, COLS], F32)
-        for g in range(G):
+
+        def load_base(g):
             rows = base[g].rearrange("(p t) n -> p (t n)", t=PACK).rearrange("p (s h i) -> h p s i", h=HALVES, i=COLS)
             for h in range(HALVES):
                 nc.sync.dma_start(out=base_sb[half(h), g].rearrange("p t c i -> p (t c) i"), in_=rows[h])
@@ -75,7 +79,7 @@ def tile_rows_pl_tnmagnitude_kernel(tc, x, w1, w2, th, dx, og, base, out_0, out_
         warm_in = sbuf("warm_in", [P, 1], F32)
         warm_out = sbuf("warm_out", [P, 1], F32)
         nc.vector.memset(warm_in[:], 1.0)
-        nc.scalar.activation(out=warm_out[:], in_=warm_in[:], func=ACT.Abs_reciprocal_sqrt)
+        nc.scalar.activation(out=warm_out[:], in_=warm_in[:], func=ACT.Ln)
 
         neg_thr = sbuf("neg_thr", [P, G, PACK], F32)
 
@@ -137,6 +141,7 @@ def tile_rows_pl_tnmagnitude_kernel(tc, x, w1, w2, th, dx, og, base, out_0, out_
         zg = per_chunk("zg", [2, COLS])
         prod = per_chunk("prod", [2, COLS])
         ssq = per_chunk("ssq", [COLS])
+        lnq = per_chunk("lnq", [COLS])
         inv = per_chunk("inv", [COLS])
         mag = per_chunk("mag", [COLS])
         num = per_chunk("num", [COLS])
@@ -172,14 +177,16 @@ def tile_rows_pl_tnmagnitude_kernel(tc, x, w1, w2, th, dx, og, base, out_0, out_
                 t = 2 * a + b
                 nc.scalar.activation(out=zg[c][:, g, t], in_=banks[g, c, a][:, b], func=ACT.Copy, scale=gain[:, g, t : t + 1])
 
+        def scale_z_vector(g, c, a):
+            for b in range(2):
+                t = 2 * a + b
+                nc.vector.tensor_scalar(out=zg[c][:, g, t], in0=banks[g, c, a][:, b], scalar1=gain[:, g, t : t + 1], scalar2=None, op0=ALU.mult)
+
         def sum_squares(part):
             nc.vector.tensor_tensor(out=view(ssq, part), in0=term(sq, part, 0), in1=term(sq, part, 1), op=ALU.add)
 
-        def inverse_root(part):
-            nc.scalar.activation(out=view(inv, part), in_=view(ssq, part), func=ACT.Abs_reciprocal_sqrt, bias=FLOOR)
-
-        def magnitude(part):
-            nc.vector.scalar_tensor_tensor(out=view(mag, part), in0=view(ssq, part), scalar=FLOOR, in1=view(inv, part), op0=ALU.add, op1=ALU.mult)
+        def logarithm(part):
+            nc.scalar.activation(out=view(lnq, part), in_=view(ssq, part), func=ACT.Ln, bias=FLOOR)
 
         def cross(g, c, a):
             pair = slice(2 * a, 2 * a + 2)
@@ -190,22 +197,24 @@ def tile_rows_pl_tnmagnitude_kernel(tc, x, w1, w2, th, dx, og, base, out_0, out_
 
         def sigmoid(part):
             c, gs, ts, cols = part
+            nc.scalar.activation(out=view(mag, part), in_=view(lnq, part), func=ACT.Exp, scale=0.5)
+            nc.scalar.activation(out=view(inv, part), in_=view(lnq, part), func=ACT.Exp, scale=-0.5)
             for g in range(gs.start, gs.stop):
                 for t in range(ts.start, ts.stop):
-                    nc.scalar.activation(out=gate[c][:, g, t], in_=mag[c][:, g, t], func=ACT.Sigmoid, bias=neg_thr[:, g, t : t + 1])
+                    nc.scalar.activation(out=gate[c][:, g, t], in_=mag[c][:, g, t], func=ACT.Tanh, scale=0.5, bias=neg_thr[:, g, t : t + 1])
 
         def rest_factor(part):
-            nc.vector.scalar_tensor_tensor(out=view(rest, part), in0=view(inv, part), scalar=1.0, in1=view(gate, part), op0=ALU.add, op1=ALU.subtract)
+            nc.vector.scalar_tensor_tensor(out=view(rest, part), in0=view(gate, part), scalar=-0.5, in1=view(inv, part), op0=ALU.mult, op1=ALU.add)
 
         def gated_numerator(part):
-            nc.vector.tensor_tensor(out=view(numg, part), in0=view(num, part), in1=view(gate, part), op=ALU.mult)
+            nc.vector.scalar_tensor_tensor(out=view(numg, part), in0=view(gate, part), scalar=1.0, in1=view(num, part), op0=ALU.add, op1=ALU.mult)
 
         def gated_change(part):
-            nc.vector.tensor_tensor(out=view(change, part), in0=view(numg, part), in1=view(rest, part), op=ALU.mult)
+            nc.vector.scalar_tensor_tensor(out=view(change, part), in0=view(rest, part), scalar=0.5, in1=view(numg, part), op0=ALU.add, op1=ALU.mult)
 
         def add_base(part):
             c, gs, ts, cols = part
-            nc.vector.tensor_tensor(out=view(y, part), in0=view(change, part), in1=base_sb[:, gs, ts, c, cols], op=ALU.add)
+            nc.vector.scalar_tensor_tensor(out=view(y, part), in0=view(change, part), scalar=0.5, in1=base_sb[:, gs, ts, c, cols], op0=ALU.mult, op1=ALU.add)
 
         def store_result(c, g, queues):
             rows = out_0.rearrange("(g p t) (c h i) -> g c h p t i", g=G, t=PACK, c=CHUNKS, h=HALVES)
@@ -237,6 +246,9 @@ def tile_rows_pl_tnmagnitude_kernel(tc, x, w1, w2, th, dx, og, base, out_0, out_
             interleave(nc.vector.tensor_copy, in_bf[key], in_raw[key], split, CHUNK)
 
         round_weights(0)
+        load_per_row(nc.sync, thr, th)
+        load_base(0)
+        load_base(1)
         quantize_weights(0)
         round_input(("x", 0), SCALAR_COLS)
         quantize_input(("x", 0))
@@ -252,71 +264,70 @@ def tile_rows_pl_tnmagnitude_kernel(tc, x, w1, w2, th, dx, og, base, out_0, out_
             for g in range(G):
                 step(g, c, a)
 
+        first, second = by_group(0, 0), by_group(0, 1)
         products("x", 0, 0)
         products("x", 0, 1)
-        round_input(("dx", 0), SCALAR_COLS)
-        quantize_input(("dx", 0))
-        round_input(("x", 1), 0)
-        nc.scalar.activation(out=neg_thr[:], in_=thr[:, :, 0:PACK], func=ACT.Copy, scale=-1.0)
-        square(0, 0)
-        both_groups(scale_z, 0, 0)
-        products("dx", 0, 0)
+        round_input(("x", 1), SCALAR_COLS)
         quantize_input(("x", 1))
         products("x", 1, 0)
-        products("x", 1, 1)
+        square(0, 0)
+        round_input(("dx", 0), 0)
         sum_squares(early[0])
-        round_input(("dx", 1), 0)
-        quantize_input(("dx", 1))
+        quantize_input(("dx", 0))
+        products("x", 1, 1)
+        scale_z(0, 0, 0)
         square(0, 1)
-        inverse_root(early[0])
+        scale_z(1, 0, 0)
+        products("dx", 0, 0)
+        round_input(("dx", 1), 0)
         sum_squares(early[1])
-        magnitude(early[0])
-        inverse_root(early[1])
-        both_groups(cross, 0, 0)
-        magnitude(early[1])
-        numerator(early[0])
-        sigmoid(early[0])
-        both_groups(scale_z, 0, 1)
-        products("dx", 0, 1)
-        sigmoid(early[1])
+        quantize_input(("dx", 1))
         square(1, 0)
-        both_groups(scale_z, 1, 0)
-        products("dx", 1, 0)
+        both_groups(scale_z_vector, 0, 1)
+        products("dx", 0, 1)
+        logarithm(early[0])
         square(1, 1)
-        both_groups(scale_z, 1, 1)
-        products("dx", 1, 1)
-        rest_factor(early[0])
-        gated_numerator(early[0])
-        gated_change(early[0])
-        rest_factor(early[1])
-        add_base(early[0])
         sum_squares(late[0])
-        both_groups(cross, 0, 1)
+        both_groups(scale_z_vector, 1, 0)
+        products("dx", 1, 0)
         sum_squares(late[1])
-        numerator(early[1])
-        inverse_root(late[0])
-        inverse_root(late[1])
+        logarithm(early[1])
+        logarithm(late[0])
+        scale_z(0, 1, 1)
+        logarithm(late[1])
+        scale_z(1, 1, 1)
+        nc.scalar.activation(out=neg_thr[:], in_=thr[:, :, 0:PACK], func=ACT.Copy, scale=-0.5)
+        products("dx", 1, 1)
+        both_groups(cross, 0, 0)
+        cross(0, 0, 1)
+        numerator(early[0])
+        cross(1, 0, 1)
         cross(0, 1, 0)
-        gated_numerator(early[1])
+        numerator(early[1])
         cross(1, 1, 0)
-        gated_change(early[1])
+        cross(0, 1, 1)
         numerator(late[0])
-        add_base(early[1])
-        store_result(0, 0, one)
-        store_result(0, 1, one)
-        magnitude(late[0])
-        magnitude(late[1])
-        sigmoid(third)
-        sigmoid(last)
-        round_result(nc.scalar.copy, 0, 0)
-        round_result(nc.scalar.copy, 0, 1)
-        both_groups(cross, 1, 1)
-        rest_factor(third)
+        cross(1, 1, 1)
+        for part in (first, second, third, last):
+            sigmoid(part)
+        rest_factor(first)
         numerator(late[1])
-        rest_factor(last)
+        gated_numerator(first)
+        rest_factor(second)
+        gated_change(first)
+        gated_numerator(second)
+        add_base(first)
+        store_result(0, 0, one)
+        round_result(nc.scalar.copy, 0, 0)
+        gated_change(second)
+        rest_factor(third)
+        add_base(second)
+        store_result(0, 1, one)
+        round_result(nc.scalar.copy, 0, 1)
         gated_numerator(third)
-        quantize_result(0, 0)
+        rest_factor(last)
         gated_change(third)
+        quantize_result(0, 0)
         quantize_result(0, 1)
         store_planes(0, one)
         add_base(third)

@@ -182,8 +182,8 @@ def tile_rows_pl_tnmagnitude_kernel(tc, x, w1, w2, th, dx, og, base, out_0, out_
                 t = 2 * a + b
                 nc.vector.tensor_scalar(out=zg[c][:, g, t], in0=banks[g, c, a][:, b], scalar1=gain[:, g, t : t + 1], scalar2=None, op0=ALU.mult)
 
-        def sum_squares(part):
-            nc.vector.tensor_tensor(out=view(ssq, part), in0=term(sq, part, 0), in1=term(sq, part, 1), op=ALU.add)
+        def sum_squares(part, engine=nc.vector):
+            engine.tensor_tensor(out=view(ssq, part), in0=term(sq, part, 0), in1=term(sq, part, 1), op=ALU.add)
 
         def logarithm(part):
             nc.scalar.activation(out=view(lnq, part), in_=view(ssq, part), func=ACT.Ln, bias=FLOOR)
@@ -192,8 +192,8 @@ def tile_rows_pl_tnmagnitude_kernel(tc, x, w1, w2, th, dx, og, base, out_0, out_
             pair = slice(2 * a, 2 * a + 2)
             nc.vector.tensor_tensor(out=prod[c][:, g, pair], in0=banks[g, c, a][:], in1=zg[c][:, g, pair], op=ALU.mult)
 
-        def numerator(part):
-            nc.vector.tensor_tensor(out=view(num, part), in0=term(prod, part, 0), in1=term(prod, part, 1), op=ALU.add)
+        def numerator(part, engine=nc.vector):
+            engine.tensor_tensor(out=view(num, part), in0=term(prod, part, 0), in1=term(prod, part, 1), op=ALU.add)
 
         def sigmoid(part):
             c, gs, ts, cols = part
@@ -277,37 +277,37 @@ def tile_rows_pl_tnmagnitude_kernel(tc, x, w1, w2, th, dx, og, base, out_0, out_
         products("x", 1, 1)
         scale_z(0, 0, 0)
         square(0, 1)
-        scale_z(1, 0, 0)
+        scale_z_vector(1, 0, 0)
         products("dx", 0, 0)
-        round_input(("dx", 1), 0)
-        sum_squares(early[1])
-        quantize_input(("dx", 1))
-        square(1, 0)
+        nc.gpsimd.tensor_scalar(
+            out=in_bf["dx", 1][:].rearrange("p (n j) -> p n j", j=PACK),
+            in0=in_raw["dx", 1][:].rearrange("p j n -> p n j"),
+            scalar1=1.0, scalar2=0.0, op0=ALU.mult, op1=ALU.add,
+        )
         both_groups(scale_z_vector, 0, 1)
         products("dx", 0, 1)
+        square(1, 0)
+        sum_squares(early[1], nc.gpsimd)
+        both_groups(scale_z_vector, 1, 0)
         logarithm(early[0])
         square(1, 1)
-        sum_squares(late[0])
-        both_groups(scale_z_vector, 1, 0)
-        products("dx", 1, 0)
+        sum_squares(late[0], nc.gpsimd)
+        both_groups(scale_z_vector, 1, 1)
         sum_squares(late[1])
         logarithm(early[1])
         logarithm(late[0])
-        scale_z(0, 1, 1)
         logarithm(late[1])
-        scale_z(1, 1, 1)
         nc.scalar.activation(out=neg_thr[:], in_=thr[:, :, 0:PACK], func=ACT.Copy, scale=-0.5)
+        quantize_input(("dx", 1))
+        products("dx", 1, 0)
         products("dx", 1, 1)
         both_groups(cross, 0, 0)
-        cross(0, 0, 1)
-        numerator(early[0])
-        cross(1, 0, 1)
-        cross(0, 1, 0)
-        numerator(early[1])
-        cross(1, 1, 0)
-        cross(0, 1, 1)
-        numerator(late[0])
-        cross(1, 1, 1)
+        numerator(early[0], nc.gpsimd)
+        both_groups(cross, 0, 1)
+        numerator(early[1], nc.gpsimd)
+        both_groups(cross, 1, 0)
+        numerator(late[0], nc.gpsimd)
+        both_groups(cross, 1, 1)
         for part in (first, second, third, last):
             sigmoid(part)
         rest_factor(first)

from contextlib import ExitStack

import concourse.mybir as mybir

G, D, M, N = 2, 256, 256, 512
FLOPS = 4 * 2 * G * D * M * N

F32 = mybir.dt.float32
BF16 = mybir.dt.bfloat16
I32 = mybir.dt.int32
U32 = mybir.dt.uint32
U8 = mybir.dt.uint8
FP8X4 = mybir.dt.float8_e4m3fn_x4
ACT = mybir.ActivationFunctionType
ALU = mybir.AluOpType

P = 128
ROWS = 64
PACK = 4
COLS = 128
HALVES = 2
CHUNK = HALVES * COLS
CHUNKS = N // CHUNK
PAIRS = PACK // 2
FLOOR = 0.05
SLOTS = 2 * PACK + 1
SCALAR_COLS = 88
SCALAR_Q = 20


def tile_rows_pl_tnmagnitude_kernel(tc, x, w1, w2, th, dx, og, base, out_0, out_1, out_2):
    nc = tc.nc
    chunks = [(g, c) for c in range(CHUNKS) for g in range(G)]

    def packed_rows(src):
        return src.rearrange("g (p j) n -> (g p) j n", j=PACK)

    def half(h):
        return slice(ROWS * h, ROWS * (h + 1))

    with ExitStack() as ctx:
        sb = ctx.enter_context(tc.tile_pool(name="sb", bufs=1))
        ps = ctx.enter_context(tc.psum_pool(name="ps", bufs=1))
        ctx.enter_context(tc.manual_schedule())

        def sbuf(name, shape, dtype):
            return sb.tile(shape, dtype, name=name, align_bytes=64)

        def per_chunk(name, shape):
            return [sbuf("%s%d" % (name, c), [P, G, PACK] + shape, F32) for c in range(CHUNKS)]

        gain = sbuf("gain", [P, G, 8], F32)
        thr = sbuf("thr", [P, G, 8], F32)

        def load_per_row(queue, dst, src):
            for h in range(HALVES):
                queue.dma_start(out=dst[half(h), :, 0:PACK], in_=src.rearrange("g (p t) o -> p g (t o)", t=PACK))

        w_raw = [sbuf("w_raw%d" % k, [P, PACK, M], F32) for k in range(2)]
        in_raw = {(name, c): sbuf("%s_raw%d" % (name, c), [P, PACK, CHUNK], F32) for name in ("x", "dx") for c in range(CHUNKS)}

        def load_input(name, src, c):
            nc.sync.dma_start(out=in_raw[name, c][:], in_=packed_rows(src)[:, :, CHUNK * c : CHUNK * (c + 1)])

        nc.sync.dma_start(out=w_raw[0][:], in_=packed_rows(w1))
        load_input("x", x, 0)
        nc.sync.dma_start(out=w_raw[1][:], in_=packed_rows(w2))
        load_per_row(nc.sync, gain, og)
        load_input("x", x, 1)
        load_input("dx", dx, 0)
        load_input("dx", dx, 1)
        base_sb = sbuf("base", [P, G, PACK, CHUNKS, COLS], F32)

        def load_base(g):
            rows = base[g].rearrange("(p t) n -> p (t n)", t=PACK).rearrange("p (s h i) -> h p s i", h=HALVES, i=COLS)
            for h in range(HALVES):
                nc.sync.dma_start(out=base_sb[half(h), g].rearrange("p t c i -> p (t c) i"), in_=rows[h])

        warm_in = sbuf("warm_in", [P, 1], F32)
        warm_out = sbuf("warm_out", [P, 1], F32)
        nc.vector.memset(warm_in[:], 1.0)
        nc.scalar.activation(out=warm_out[:], in_=warm_in[:], func=ACT.Ln)

        neg_thr = sbuf("neg_thr", [P, G, PACK], F32)

        w_codes = [sbuf("w_codes%d" % k, [P, SLOTS * ROWS], U32) for k in range(2)]
        w_scales = [sbuf("w_scales%d" % k, [P, SLOTS * ROWS], U8) for k in range(2)]
        w_bf = [sbuf("w_bf%d" % k, [P, PACK, ROWS * PACK], BF16) for k in range(2)]
        for k in range(2):
            nc.vector.memset(w_codes[k][:], 0)
            nc.vector.memset(w_scales[k][:].bitcast(U32), 0)

        def round_weights(k):
            dst = w_bf[k][:].rearrange("p (a b) (q j) -> p a q j b", b=2, j=PACK)
            src = w_raw[k][:].rearrange("p j (q a b) -> p a q j b", a=PAIRS, b=2)
            nc.scalar.copy(out=dst[:, :, 0:SCALAR_Q], in_=src[:, :, 0:SCALAR_Q])
            nc.vector.tensor_copy(out=dst[:, :, SCALAR_Q:], in_=src[:, :, SCALAR_Q:])

        def quantize_weights(k):
            for t in range(PACK):
                slot = slice(ROWS * (2 * t + 1), ROWS * (2 * t + 2))
                nc.vector.quantize_mx(out=w_codes[k][:, slot].bitcast(FP8X4), scales=w_scales[k][:, slot], in_=w_bf[k][:, t, :])

        def interleave(copy, dst, src, lo, hi):
            copy(
                out=dst[:, PACK * lo : PACK * hi].rearrange("p (c i j) -> p c j i", i=4, j=PACK),
                in_=src[:, :, lo:hi].rearrange("p j (c i) -> p c j i", i=4),
            )

        in_bf = {key: sbuf("%s_bf%d" % key, [P, CHUNK * PACK], BF16) for key in in_raw}
        in_codes = {key: sbuf("%s_codes%d" % key, [P, CHUNK], U32) for key in in_raw}
        in_scales = {key: sbuf("%s_scales%d" % key, [P, CHUNK], U8) for key in in_raw}

        def quantize_input(key):
            nc.vector.quantize_mx(out=in_codes[key][:].bitcast(FP8X4), scales=in_scales[key][:], in_=in_bf[key][:])

        banks = {(g, c, a): ps.tile([P, 2, 2, COLS], F32, name="bank_%d_%d_%d" % (g, c, a)) for g, c in chunks for a in range(PAIRS)}

        def product_pass(name, g, c, a, b, k, h):
            start = ROWS * (2 * (2 * a + b) + 1 - h)
            window = slice(start, start + P)
            cols = slice(COLS * h, COLS * (h + 1))
            nc.tensor.matmul_mx(
                out=banks[g, c, a][:, b, k, :],
                lhsT=w_codes[k][half(g), window].bitcast(FP8X4),
                lhsT_scale=w_scales[k][half(g), window],
                rhs=in_codes[name, c][half(g), cols].bitcast(FP8X4),
                rhs_scale=in_scales[name, c][half(g), cols],
                start=(h == 0),
                stop=(h == HALVES - 1),
            )

        passes = [(k, b, h) for k in range(2) for b in range(2) for h in range(HALVES)]

        def products(name, c, a):
            for k, b, h in passes:
                for g in range(G):
                    product_pass(name, g, c, a, b, k, h)

        sq = per_chunk("sq", [2, COLS])
        zg = per_chunk("zg", [2, COLS])
        prod = per_chunk("prod", [2, COLS])
        ssq = per_chunk("ssq", [COLS])
        lnq = per_chunk("lnq", [COLS])
        inv = per_chunk("inv", [COLS])
        mag = per_chunk("mag", [COLS])
        num = per_chunk("num", [COLS])
        gate = per_chunk("gate", [COLS])
        rest = per_chunk("rest", [COLS])
        numg = per_chunk("numg", [COLS])
        change = per_chunk("change", [COLS])
        y = per_chunk("y", [COLS])
        y_bf = [sbuf("y_bf%d" % c, [P, G, COLS * PACK], BF16) for c in range(CHUNKS)]
        y_codes = [sbuf("y_codes%d" % c, [P, G, COLS], U32) for c in range(CHUNKS)]
        y_scales = [sbuf("y_scales%d" % c, [P, G, COLS], U8) for c in range(CHUNKS)]

        def by_pair(c, a):
            return (c, slice(0, G), slice(2 * a, 2 * a + 2), slice(0, COLS))

        def by_group(c, g, lo=0, hi=COLS):
            return (c, slice(g, g + 1), slice(0, PACK), slice(lo, hi))

        def view(tiles, part):
            c, gs, ts, cols = part
            return tiles[c][:, gs, ts, cols]

        def term(tiles, part, k):
            c, gs, ts, cols = part
            return tiles[c][:, gs, ts, k, cols]

        def square(c, a):
            for g in range(G):
                nc.scalar.activation(out=sq[c][:, g, 2 * a : 2 * a + 2], in_=banks[g, c, a][:], func=ACT.Square)

        def scale_z(g, c, a):
            for b in range(2):
                t = 2 * a + b
                nc.scalar.activation(out=zg[c][:, g, t], in_=banks[g, c, a][:, b], func=ACT.Copy, scale=gain[:, g, t : t + 1])

        def scale_z_vector(g, c, a):
            for b in range(2):
                t = 2 * a + b
                nc.vector.tensor_scalar(out=zg[c][:, g, t], in0=banks[g, c, a][:, b], scalar1=gain[:, g, t : t + 1], scalar2=None, op0=ALU.mult)

        def sum_squares(part, engine=nc.vector):
            engine.tensor_tensor(out=view(ssq, part), in0=term(sq, part, 0), in1=term(sq, part, 1), op=ALU.add)

        def logarithm(part):
            nc.scalar.activation(out=view(lnq, part), in_=view(ssq, part), func=ACT.Ln, bias=FLOOR)

        def cross(g, c, a):
            pair = slice(2 * a, 2 * a + 2)
            nc.vector.tensor_tensor(out=prod[c][:, g, pair], in0=banks[g, c, a][:], in1=zg[c][:, g, pair], op=ALU.mult)

        def numerator(part, engine=nc.vector):
            engine.tensor_tensor(out=view(num, part), in0=term(prod, part, 0), in1=term(prod, part, 1), op=ALU.add)

        def sigmoid(part):
            c, gs, ts, cols = part
            nc.scalar.activation(out=view(mag, part), in_=view(lnq, part), func=ACT.Exp, scale=0.5)
            nc.scalar.activation(out=view(inv, part), in_=view(lnq, part), func=ACT.Exp, scale=-0.5)
            for g in range(gs.start, gs.stop):
                for t in range(ts.start, ts.stop):
                    nc.scalar.activation(out=gate[c][:, g, t], in_=mag[c][:, g, t], func=ACT.Tanh, scale=0.5, bias=neg_thr[:, g, t : t + 1])

        def rest_factor(part):
            nc.vector.scalar_tensor_tensor(out=view(rest, part), in0=view(gate, part), scalar=-0.5, in1=view(inv, part), op0=ALU.mult, op1=ALU.add)

        def gated_numerator(part):
            nc.vector.scalar_tensor_tensor(out=view(numg, part), in0=view(gate, part), scalar=1.0, in1=view(num, part), op0=ALU.add, op1=ALU.mult)

        def gated_change(part):
            nc.vector.scalar_tensor_tensor(out=view(change, part), in0=view(rest, part), scalar=0.5, in1=view(numg, part), op0=ALU.add, op1=ALU.mult)

        def add_base(part):
            c, gs, ts, cols = part
            nc.vector.scalar_tensor_tensor(out=view(y, part), in0=view(change, part), scalar=0.5, in1=base_sb[:, gs, ts, c, cols], op0=ALU.mult, op1=ALU.add)

        def store_result(c, g, queues):
            rows = out_0.rearrange("(g p t) (c h i) -> g c h p t i", g=G, t=PACK, c=CHUNKS, h=HALVES)
            for h in range(HALVES):
                queues[h].dma_start(out=rows[g, c, h], in_=y[c][half(h), g])

        def round_result(copy, c, g, lo=0, hi=COLS):
            interleave(copy, y_bf[c][:, g], y[c][:, g], lo, hi)

        def quantize_result(c, g):
            nc.vector.quantize_mx(out=y_codes[c][:, g].bitcast(FP8X4), scales=y_scales[c][:, g], in_=y_bf[c][:, g])

        def store_planes(c, queues):
            words = out_1[0].rearrange("p n u -> p (n u)").bitcast(I32).rearrange("(g p) (c h i) -> c h p g i", g=G, c=CHUNKS, h=HALVES)
            for h in range(HALVES):
                queues[h].dma_start(out=words[c, h], in_=y_codes[c][half(h)].bitcast(I32))
            rows = out_2[0].bitcast(I32).rearrange("(g q r) (c h i) -> c h q r g i", g=G, q=2, c=CHUNKS, h=HALVES)
            for h in range(HALVES):
                for q in range(2):
                    first = ROWS * h + 32 * q
                    queues[h].dma_start(out=rows[c, h, q], in_=y_scales[c][first : first + 4].bitcast(I32))

        both = (nc.sync, nc.scalar)
        one = (nc.sync, nc.sync)

        def round_input(key, split):
            if split:
                interleave(nc.scalar.copy, in_bf[key], in_raw[key], 0, split)
            interleave(nc.vector.tensor_copy, in_bf[key], in_raw[key], split, CHUNK)

        round_weights(0)
        load_per_row(nc.sync, thr, th)
        load_base(0)
        load_base(1)
        quantize_weights(0)
        round_input(("x", 0), SCALAR_COLS)
        quantize_input(("x", 0))
        round_weights(1)
        quantize_weights(1)

        early = [by_pair(0, a) for a in range(PAIRS)]
        late = [by_pair(1, a) for a in range(PAIRS)]
        third, last = by_group(1, 0), by_group(1, 1)
        last_halves = [by_group(1, 1, 0, COLS // 2), by_group(1, 1, COLS // 2, COLS)]

        def both_groups(step, c, a):
            for g in range(G):
                step(g, c, a)

        first, second = by_group(0, 0), by_group(0, 1)
        products("x", 0, 0)
        products("x", 0, 1)
        round_input(("x", 1), SCALAR_COLS)
        quantize_input(("x", 1))
        products("x", 1, 0)
        square(0, 0)
        round_input(("dx", 0), 0)
        sum_squares(early[0])
        quantize_input(("dx", 0))
        products("x", 1, 1)
        scale_z(0, 0, 0)
        square(0, 1)
        scale_z_vector(1, 0, 0)
        products("dx", 0, 0)
        nc.gpsimd.tensor_scalar(
            out=in_bf["dx", 1][:].rearrange("p (n j) -> p n j", j=PACK),
            in0=in_raw["dx", 1][:].rearrange("p j n -> p n j"),
            scalar1=1.0, scalar2=0.0, op0=ALU.mult, op1=ALU.add,
        )
        both_groups(scale_z_vector, 0, 1)
        products("dx", 0, 1)
        square(1, 0)
        sum_squares(early[1], nc.gpsimd)
        both_groups(scale_z_vector, 1, 0)
        logarithm(early[0])
        square(1, 1)
        sum_squares(late[0], nc.gpsimd)
        both_groups(scale_z_vector, 1, 1)
        sum_squares(late[1])
        logarithm(early[1])
        logarithm(late[0])
        logarithm(late[1])
        nc.scalar.activation(out=neg_thr[:], in_=thr[:, :, 0:PACK], func=ACT.Copy, scale=-0.5)
        quantize_input(("dx", 1))
        products("dx", 1, 0)
        products("dx", 1, 1)
        both_groups(cross, 0, 0)
        numerator(early[0], nc.gpsimd)
        both_groups(cross, 0, 1)
        numerator(early[1], nc.gpsimd)
        both_groups(cross, 1, 0)
        numerator(late[0], nc.gpsimd)
        both_groups(cross, 1, 1)
        for part in (first, second, third, last):
            sigmoid(part)
        rest_factor(first)
        numerator(late[1])
        gated_numerator(first)
        rest_factor(second)
        gated_change(first)
        gated_numerator(second)
        add_base(first)
        store_result(0, 0, one)
        round_result(nc.scalar.copy, 0, 0)
        gated_change(second)
        rest_factor(third)
        add_base(second)
        store_result(0, 1, one)
        round_result(nc.scalar.copy, 0, 1)
        gated_numerator(third)
        rest_factor(last)
        gated_change(third)
        quantize_result(0, 0)
        quantize_result(0, 1)
        store_planes(0, one)
        add_base(third)
        store_result(1, 0, both)
        round_result(nc.scalar.copy, 1, 0)
        for part in last_halves:
            gated_numerator(part)
        for part in last_halves:
            gated_change(part)
        add_base(last_halves[0])
        round_result(nc.scalar.copy, 1, 1, 0, COLS // 2)
        add_base(last_halves[1])
        quantize_result(1, 0)
        round_result(nc.vector.tensor_copy, 1, 1, COLS // 2, COLS)
        store_result(1, 1, both)
        quantize_result(1, 1)
        store_planes(1, both)
